import numpy as np
import ml_dtypes


def mxq(x, axis, fmt="e4m3"):
    dtype, down = {"e4m3": (ml_dtypes.float8_e4m3fn, 7), "e5m2": (ml_dtypes.float8_e5m2, 14)}[fmt]
    v = np.moveaxis(np.asarray(x, np.float32).astype(ml_dtypes.bfloat16).astype(np.float64), axis, -1)
    blocks = v.reshape(v.shape[:-1] + (-1, 32))
    amax = np.abs(blocks).max(-1, keepdims=True)
    byte = np.maximum(np.where(amax > 0, np.frexp(amax)[1] - 1 + 127, 0) - down, 1)
    scale = np.exp2(byte - 127.0)
    codes = (blocks / scale).astype(np.float32).astype(dtype).astype(np.float64)
    return np.moveaxis((codes * scale).reshape(v.shape), -1, axis)


WIDE = False


def mx_kscale(k):
    if not WIDE:
        return np.ones(k)
    levels = np.array([10, -10, 5, -5, 0])
    if k % 512:
        return np.exp2(np.random.permutation(np.resize(levels, k // 32))).repeat(32)
    a = np.empty((k // 512, 16))
    for p in range(k // 512):
        a[p, :8] = np.random.permutation(np.resize(levels, 8))
        for g in range(8):
            far = levels[np.abs(levels - a[p, g]) >= 10]
            a[p, g + 8] = far[np.random.randint(len(far))]
    return np.exp2(a.ravel()).repeat(32)


def f64(x):
    return np.asarray(x).astype(np.float64)


def striped(idx):
    return np.tile(idx.reshape(-1, 16).T, (8, 1)).astype(np.uint16)


def unstriped(offs):
    return offs[:16].T.reshape(-1).astype(np.int64)


def striped8(idx):
    return np.concatenate([x.reshape(-1, 16).T for x in idx]).astype(np.uint16)


def runs(offs, k):
    lists = np.stack([offs[16 * r : 16 * r + 16].T.reshape(-1) for r in range(8)]).astype(np.int64)
    return lists[np.arange(k) % 512 // 64]


def pack_weight(w):
    k, n = w.shape
    w = f64(np.asarray(w, np.float32).astype(ml_dtypes.bfloat16)).reshape(k // 32, 32, n)
    amax = np.abs(w).max(1)
    byte = np.clip(np.where(amax > 0, np.frexp(amax)[1] - 1 + 127 - 7, 1), 1, 254)
    scaled = (w * np.exp2(127.0 - byte)[:, None, :]).reshape(k, n).astype(np.float32)
    words = np.ascontiguousarray(scaled.reshape(k // 512, 128, 4, n).transpose(0, 1, 3, 2)).astype(ml_dtypes.float8_e4m3fn).view(np.uint8)
    return words, np.ascontiguousarray(byte.astype(np.uint8).reshape(k // 512, 16, n))


def unpack_weight(words, scales):
    g, p, n, _ = words.shape
    vals = np.ascontiguousarray(words).view(ml_dtypes.float8_e4m3fn).astype(np.float64) * np.repeat(np.exp2(scales.astype(np.float64) - 127.0), 8, axis=1)[..., None]
    return vals.transpose(0, 1, 3, 2).reshape(g * 512, n)


E2M1 = np.array([0.0, 0.5, 1.0, 1.5, 2.0, 3.0, 4.0, 6.0, -0.0, -0.5, -1.0, -1.5, -2.0, -3.0, -4.0, -6.0])


def pack_fp4(w):
    k, n = w.shape
    w = f64(np.asarray(w, np.float32).astype(ml_dtypes.bfloat16)).reshape(k // 32, 32, n)
    amax = np.abs(w).max(1)
    mant, ex = np.frexp(amax / 6.0)
    byte = np.clip(np.where(amax > 0, np.where(mant > 0.5, ex, ex - 1) + 127, 1), 1, 254)
    scaled = (w * np.exp2(127.0 - byte)[:, None, :]).reshape(k, n).astype(np.float32)
    c = np.ascontiguousarray(scaled.reshape(k // 512, 128, 4, n).transpose(0, 1, 3, 2)).astype(ml_dtypes.float4_e2m1fn).view(np.uint8) & 0xF
    words = (c[..., 0::2] | (c[..., 1::2] << 4)).reshape(k // 512, 128, 2 * n)
    return np.ascontiguousarray(words), np.ascontiguousarray(byte.astype(np.uint8).reshape(k // 512, 16, n))


def unpack_fp4(words, scales):
    g, _, n = scales.shape
    words = np.ascontiguousarray(words).reshape(g, 128, n, 2)
    nib = np.empty((g, 128, n, 4), np.uint8)
    nib[..., 0::2] = words & 0xF
    nib[..., 1::2] = words >> 4
    vals = E2M1[nib] * np.repeat(np.exp2(scales.astype(np.float64) - 127.0), 8, axis=1)[..., None]
    return vals.transpose(0, 1, 3, 2).reshape(g * 512, n)


def planes(y):
    n, m = y.shape
    v = y.astype(np.float32).astype(ml_dtypes.bfloat16).astype(np.float64).reshape(n // 32, 32, m)
    top = np.abs(v).max(1)
    byte = np.clip(np.where(top > 0, np.frexp(top)[1] - 1 + 127 - 7, 1), 1, 254)
    codes = (v * np.exp2(127.0 - byte)[:, None, :]).reshape(n, m).astype(np.float32).astype(ml_dtypes.float8_e4m3fn).view(np.uint8)
    words = codes.reshape(n // 512, 128, 4, m).transpose(0, 1, 3, 2)
    return np.ascontiguousarray(words), np.ascontiguousarray(byte.astype(np.uint8).reshape(n // 512, 16, m))


K, T, S, N, H = 512, 2048, 512, 512, 512


def setup_inputs():
    n = np.random.standard_normal
    s = mx_kscale(K)[:, None]
    u = mx_kscale(H)
    packed_xT = pack_weight(n((K, T)) * s)
    packed_w1 = pack_fp4(n((K, H)) / np.sqrt(K) / s)
    packed_w2 = pack_fp4(n((H, N)) / np.sqrt(H) / u[:, None])
    return {
        "x_words": packed_xT[0],
        "x_scales": packed_xT[1],
        "w1_words": packed_w1[0],
        "w1_scales": packed_w1[1],
        "gn": (np.random.uniform(0.5, 1.5, (H, 1)) * u[:, None]).astype(np.float32),
        "w2_words": packed_w2[0],
        "w2_scales": packed_w2[1],
        "offs": striped(np.random.permutation(T)[:S]),
        "n1": striped8(np.stack([np.random.permutation(S) for _ in range(8)])),
        "n2": striped8(np.stack([np.random.permutation(S) for _ in range(8)])),
        "n3": striped8(np.stack([np.random.permutation(S) for _ in range(8)])),
        "n4": striped8(np.stack([np.random.permutation(S) for _ in range(8)])),
    }


def reference(x_words, x_scales, w1_words, w1_scales, gn, w2_words, w2_scales, offs, n1, n2, n3, n4):
    xq = unpack_weight(x_words, x_scales)[:, unstriped(offs)]
    y = unpack_fp4(w1_words, w1_scales).T @ xq
    z = f64(gn) * (y * (y[np.arange(H)[:, None], runs(n1, H)] - (y[np.arange(H)[:, None], runs(n2, H)])))
    h = unpack_fp4(w2_words, w2_scales).T @ mxq(z, 0, "e4m3")
    out_0 = (h - (h[np.arange(N)[:, None], runs(n3, N)])) / (np.abs(y) + np.abs(y[np.arange(H)[:, None], runs(n4, H)]) + 0.5)
    return (out_0,) + planes(out_0)

@@ -1,0 +1,203 @@
+from contextlib import ExitStack
+
+import concourse.mybir as mybir
+
+K, T, S, H, N = 512, 2048, 512, 512, 512
+FLOPS = 2 * K * H * S + 2 * H * N * S
+
+F32 = mybir.dt.float32
+BF16 = mybir.dt.bfloat16
+I32 = mybir.dt.int32
+U32 = mybir.dt.uint32
+U16 = mybir.dt.uint16
+U8 = mybir.dt.uint8
+FP8X4 = mybir.dt.float8_e4m3fn_x4
+FP4X4 = mybir.dt.float4_e2m1fn_x4
+ALU = mybir.AluOpType
+ACT = mybir.ActivationFunctionType
+
+P = 128
+PACK = 4
+HALVES = 2
+CH = S // HALVES
+LC = CH // 16
+
+
+def load_scale_rows(queue, tile, scales):
+    for q in range(4):
+        queue.dma_start(out=tile[32 * q : 32 * q + 4, :].bitcast(I32), in_=scales[0, 4 * q : 4 * q + 4, :].bitcast(I32))
+
+
+def paired_in(ap):
+    return ap.rearrange("p t (c i) -> p c t i", i=2)
+
+
+def paired_out(ap):
+    return ap.rearrange("p (c i t) -> p c t i", i=2, t=PACK)
+
+
+def tile_picked_skipnormbwind_none_po_kernel(
+    tc, x_words, x_scales, w1_words, w1_scales, gn, w2_words, w2_scales, offs, n1, n2, n3, n4, out_0, out_1, out_2
+):
+    nc = tc.nc
+    with ExitStack() as ctx:
+        sb = ctx.enter_context(tc.tile_pool(name="sb", bufs=1))
+        ps = ctx.enter_context(tc.psum_pool(name="ps", bufs=1))
+
+        def tiles(name, count, shape, dtype):
+            return [sb.tile(shape, dtype, name="%s%d" % (name, i), align_bytes=64) for i in range(count)]
+
+        offs_t = sb.tile([P, S // 16], U16, name="offs_t")
+        n1_t = sb.tile([P, S // 16], U16, name="n1_t")
+        n2_t = sb.tile([P, S // 16], U16, name="n2_t")
+        n3_t = sb.tile([P, S // 16], U16, name="n3_t")
+        n4_t = sb.tile([P, S // 16], U16, name="n4_t")
+        xw = sb.tile([P, T], U32, name="xw", align_bytes=64)
+        xs = sb.tile([P, T], U8, name="xs", align_bytes=64)
+        w1w_raw = sb.tile([P, 2 * H], U8, name="w1w_raw", align_bytes=64)
+        w2w_raw = sb.tile([P, 2 * N], U8, name="w2w_raw", align_bytes=64)
+        w1s_raw = sb.tile([P, H], U8, name="w1s_raw", align_bytes=64)
+        w2s_raw = sb.tile([P, N], U8, name="w2s_raw", align_bytes=64)
+        w1w = sb.tile([P, 2 * H], U8, name="w1w", align_bytes=64)
+        w2w = sb.tile([P, 2 * N], U8, name="w2w", align_bytes=64)
+        w1s = sb.tile([P, H], U8, name="w1s", align_bytes=64)
+        w2s = sb.tile([P, N], U8, name="w2s", align_bytes=64)
+        gain = sb.tile([P, PACK], F32, name="gain")
+        warm_in = sb.tile([P, 1], F32, name="warm_in")
+        warm_out = sb.tile([P, 1], F32, name="warm_out")
+
+        nc.vector.memset(xs[:].bitcast(I32), 0)
+        nc.vector.memset(w1s_raw[:].bitcast(I32), 0)
+        nc.gpsimd.memset(w2s_raw[:].bitcast(I32), 0)
+        nc.vector.memset(warm_in[:], 1.0)
+        nc.scalar.activation(warm_out[:], warm_in[:], ACT.Abs_reciprocal_sqrt)
+
+        load_scale_rows(nc.sync, xs, x_scales)
+        nc.sync.dma_start(offs_t[:], offs)
+        nc.sync.dma_start(out=w1w_raw[:].bitcast(I32), in_=w1_words[0].bitcast(I32))
+        nc.sync.dma_start(n2_t[:], n2)
+        nc.sync.dma_start(out=xw[:].bitcast(I32), in_=x_words[0].rearrange("p n t -> p (n t)").bitcast(I32))
+        load_scale_rows(nc.sync, w1s_raw, w1_scales)
+        nc.sync.dma_start(out=w2w_raw[:].bitcast(I32), in_=w2_words[0].bitcast(I32))
+        nc.sync.dma_start(n1_t[:], n1)
+        load_scale_rows(nc.sync, w2s_raw, w2_scales)
+        nc.sync.dma_start(out=gain[:], in_=gn.rearrange("(p t) o -> p (t o)", t=PACK))
+        nc.sync.dma_start(n4_t[:], n4)
+        nc.sync.dma_start(n3_t[:], n3)
+
+        def deal_words(dst, src):
+            nc.vector.tensor_copy(
+                out=dst[:].rearrange("p (t m b) -> p t m b", t=PACK, b=2),
+                in_=src[:].rearrange("p (m t b) -> p t m b", t=PACK, b=2),
+            )
+
+        def deal_scales(dst, src):
+            nc.vector.tensor_copy(
+                out=dst[:].rearrange("p (t m) -> p t m", t=PACK),
+                in_=src[:].rearrange("p (m t) -> p t m", t=PACK),
+            )
+
+        def part(lst, c):
+            return lst[:, c * LC : (c + 1) * LC]
+
+        xsg = sb.tile([P, S], U8, name="xsg", align_bytes=64)
+        xg = tiles("xg", HALVES, [P, CH], U32)
+        nc.vector.tensor_copy(xsg[:], xs[:].indirect(offs_t[:]))
+        deal_words(w1w, w1w_raw)
+        deal_scales(w1s, w1s_raw)
+        for c in range(HALVES):
+            nc.vector.tensor_copy(xg[c][:], xw[:].indirect(part(offs_t, c)))
+        deal_words(w2w, w2w_raw)
+        deal_scales(w2s, w2s_raw)
+
+        def product(name, ww, ws, codes, scales, t, c):
+            acc = ps.tile([P, CH], F32, name="%s%d_%d" % (name, t, c), tag="bank%d_%d" % (t, c))
+            nc.tensor.matmul_mx(
+                out=acc[:],
+                lhsT=ww[:, 2 * P * t : 2 * P * (t + 1)].bitcast(FP4X4),
+                lhsT_scale=ws[:, P * t : P * (t + 1)],
+                rhs=codes.bitcast(FP8X4),
+                rhs_scale=scales,
+                start=True,
+                stop=True,
+            )
+            return acc
+
+        y_ps = {}
+        y_win = tiles("y_win", PACK, [P, S], F32)
+        for c in range(HALVES):
+            for t in range(PACK):
+                y_ps[t, c] = product("y", w1w, w1s, xg[c][:], xsg[:, c * CH : (c + 1) * CH], t, c)
+                nc.scalar.copy(y_win[t][:, c * CH : (c + 1) * CH], y_ps[t, c][:])
+
+        gy = tiles("gy", HALVES, [P, PACK, CH], F32)
+        a_win = tiles("a_win", PACK, [P, S], F32)
+        a_own = tiles("a_own", HALVES, [P, PACK, CH], F32)
+        for c in range(HALVES):
+            for t in range(PACK):
+                nc.scalar.activation(gy[c][:, t, :], y_ps[t, c][:], ACT.Copy, scale=gain[:, t : t + 1])
+        for c in range(HALVES):
+            for t in range(PACK):
+                nc.scalar.activation(a_win[t][:, c * CH : (c + 1) * CH], y_ps[t, c][:], ACT.Abs)
+                nc.scalar.activation(a_own[c][:, t, :], y_ps[t, c][:], ACT.Abs)
+
+        y2 = tiles("y2_", HALVES, [P, PACK, CH], F32)
+        diff = tiles("diff", HALVES, [P, PACK, CH], F32)
+        zb = tiles("zb", HALVES, [P, PACK * CH], BF16)
+        zq = tiles("zq", HALVES, [P, CH], U32)
+        zs = tiles("zs", HALVES, [P, CH], U8)
+        h_win = tiles("h_win", PACK, [P, S], F32)
+        h_own = tiles("h_own", HALVES, [P, PACK, CH], F32)
+
+        def second_product(c):
+            nc.vector.quantize_mx(out=zq[c][:].bitcast(FP8X4), scales=zs[c][:], in_=zb[c][:])
+            for t in range(PACK):
+                acc = product("h", w2w, w2s, zq[c][:], zs[c][:], t, c)
+                nc.scalar.activation(h_win[t][:, c * CH : (c + 1) * CH], acc[:], ACT.Copy, scale=-1.0)
+                nc.scalar.copy(h_own[c][:, t, :], acc[:])
+
+        for c in range(HALVES):
+            for t in range(PACK):
+                nc.vector.tensor_copy(y2[c][:, t, :], y_win[t][:].indirect(part(n2_t, c)))
+                if t == 0 and c > 0:
+                    second_product(c - 1)
+                if t > 0:
+                    nc.vector.tensor_tensor(diff[c][:, t - 1, :], y_win[t - 1][:].indirect(part(n1_t, c)), y2[c][:, t - 1, :], ALU.subtract)
+            nc.vector.tensor_tensor(diff[c][:, PACK - 1, :], y_win[PACK - 1][:].indirect(part(n1_t, c)), y2[c][:, PACK - 1, :], ALU.subtract)
+            nc.vector.tensor_tensor(paired_out(zb[c][:]), paired_in(diff[c][:]), paired_in(gy[c][:]), ALU.mult)
+
+        den = tiles("den", HALVES, [P, PACK, CH], F32)
+        root = tiles("root", HALVES, [P, PACK, CH], F32)
+        inv = tiles("inv", HALVES, [P, PACK, CH], F32)
+        for c in range(HALVES):
+            for t in range(PACK):
+                nc.vector.tensor_tensor(den[c][:, t, :], a_win[t][:].indirect(part(n4_t, c)), a_own[c][:, t, :], ALU.add)
+                if t == 0 and c == 0:
+                    second_product(HALVES - 1)
+            nc.scalar.activation(root[c][:], den[c][:], ACT.Abs_reciprocal_sqrt, bias=0.5)
+            nc.scalar.activation(inv[c][:], root[c][:], ACT.Square)
+
+        num = tiles("num", HALVES, [P, PACK, CH], F32)
+        res = tiles("res", HALVES, [P, PACK, CH], F32)
+        ob = tiles("ob", HALVES, [P, PACK * CH], BF16)
+        oq = tiles("oq", HALVES, [P, CH], U32)
+        osc = sb.tile([P, S], U8, name="osc", align_bytes=64)
+        out_rows = out_0.rearrange("(p t) j -> p t j", t=PACK)
+        out_words = out_1[0].rearrange("p n t -> p (n t)").bitcast(I32)
+
+        def planes(c):
+            nc.vector.quantize_mx(out=oq[c][:].bitcast(FP8X4), scales=osc[:, c * CH : (c + 1) * CH], in_=ob[c][:])
+            nc.sync.dma_start(out=out_words[:, c * CH : (c + 1) * CH], in_=oq[c][:].bitcast(I32))
+
+        for c in range(HALVES):
+            for t in range(PACK):
+                nc.vector.tensor_tensor(num[c][:, t, :], h_win[t][:].indirect(part(n3_t, c)), h_own[c][:, t, :], ALU.add)
+            if c > 0:
+                planes(c - 1)
+            nc.vector.tensor_tensor(res[c][:], num[c][:], inv[c][:], ALU.mult)
+            nc.sync.dma_start(out=out_rows[:, :, c * CH : (c + 1) * CH], in_=res[c][:])
+            nc.scalar.copy(paired_out(ob[c][:]), paired_in(res[c][:]))
+        planes(HALVES - 1)
+        for q in range(4):
+            queue = nc.sync if q % 2 else nc.scalar
+            queue.dma_start(out=out_2[0, 4 * q : 4 * q + 4, :].bitcast(I32), in_=osc[32 * q : 32 * q + 4, :].bitcast(I32))

@@ -18,9 +18,7 @@ ACT = mybir.ActivationFunctionType
 
 P = 128
 PACK = 4
-HALVES = 2
-CH = S // HALVES
-LC = CH // 16
+HALF = S // 2
 
 
 def load_scale_rows(queue, tile, scales):
@@ -44,8 +42,8 @@ def tile_picked_skipnormbwind_none_po_kernel(
         sb = ctx.enter_context(tc.tile_pool(name="sb", bufs=1))
         ps = ctx.enter_context(tc.psum_pool(name="ps", bufs=1))
 
-        def tiles(name, count, shape, dtype):
-            return [sb.tile(shape, dtype, name="%s%d" % (name, i), align_bytes=64) for i in range(count)]
+        def tiles(name, shape, dtype):
+            return [sb.tile(shape, dtype, name="%s%d" % (name, t), align_bytes=64) for t in range(PACK)]
 
         offs_t = sb.tile([P, S // 16], U16, name="offs_t")
         n1_t = sb.tile([P, S // 16], U16, name="n1_t")
@@ -58,10 +56,6 @@ def tile_picked_skipnormbwind_none_po_kernel(
         w2w_raw = sb.tile([P, 2 * N], U8, name="w2w_raw", align_bytes=64)
         w1s_raw = sb.tile([P, H], U8, name="w1s_raw", align_bytes=64)
         w2s_raw = sb.tile([P, N], U8, name="w2s_raw", align_bytes=64)
-        w1w = sb.tile([P, 2 * H], U8, name="w1w", align_bytes=64)
-        w2w = sb.tile([P, 2 * N], U8, name="w2w", align_bytes=64)
-        w1s = sb.tile([P, H], U8, name="w1s", align_bytes=64)
-        w2s = sb.tile([P, N], U8, name="w2s", align_bytes=64)
         gain = sb.tile([P, PACK], F32, name="gain")
         warm_in = sb.tile([P, 1], F32, name="warm_in")
         warm_out = sb.tile([P, 1], F32, name="warm_out")
@@ -80,8 +74,8 @@ def tile_picked_skipnormbwind_none_po_kernel(
         load_scale_rows(nc.sync, w1s_raw, w1_scales)
         nc.sync.dma_start(out=w2w_raw[:].bitcast(I32), in_=w2_words[0].bitcast(I32))
         nc.sync.dma_start(n1_t[:], n1)
-        load_scale_rows(nc.sync, w2s_raw, w2_scales)
         nc.sync.dma_start(out=gain[:], in_=gn.rearrange("(p t) o -> p (t o)", t=PACK))
+        load_scale_rows(nc.sync, w2s_raw, w2_scales)
         nc.sync.dma_start(n4_t[:], n4)
         nc.sync.dma_start(n3_t[:], n3)
 
@@ -91,113 +85,141 @@ def tile_picked_skipnormbwind_none_po_kernel(
                 in_=src[:].rearrange("p (m t b) -> p t m b", t=PACK, b=2),
             )
 
-        def deal_scales(dst, src):
+        def deal_scales(dst, src, t0, t1):
             nc.vector.tensor_copy(
-                out=dst[:].rearrange("p (t m) -> p t m", t=PACK),
-                in_=src[:].rearrange("p (m t) -> p t m", t=PACK),
+                out=dst[:].rearrange("p (t m) -> p t m", t=PACK)[:, t0:t1, :],
+                in_=src[:].rearrange("p (m t) -> p t m", t=PACK)[:, t0:t1, :],
             )
 
-        def part(lst, c):
-            return lst[:, c * LC : (c + 1) * LC]
-
         xsg = sb.tile([P, S], U8, name="xsg", align_bytes=64)
-        xg = tiles("xg", HALVES, [P, CH], U32)
+        xg = [sb.tile([P, HALF], U32, name="xg%d" % c, align_bytes=64) for c in range(2)]
+        w1w = sb.tile([P, 2 * H], U8, name="w1w", align_bytes=64)
+        w2w = sb.tile([P, 2 * N], U8, name="w2w", align_bytes=64)
+        w1s = sb.tile([P, H], U8, name="w1s", align_bytes=64)
+        w2s = sb.tile([P, N], U8, name="w2s", align_bytes=64)
         nc.vector.tensor_copy(xsg[:], xs[:].indirect(offs_t[:]))
         deal_words(w1w, w1w_raw)
-        deal_scales(w1s, w1s_raw)
-        for c in range(HALVES):
-            nc.vector.tensor_copy(xg[c][:], xw[:].indirect(part(offs_t, c)))
+        nc.vector.tensor_copy(xg[0][:], xw[:].indirect(offs_t[:, 0 : HALF // 16]))
+        deal_scales(w1s, w1s_raw, 0, 2)
+        nc.vector.tensor_copy(xg[1][:], xw[:].indirect(offs_t[:, HALF // 16 : S // 16]))
+        deal_scales(w1s, w1s_raw, 2, PACK)
         deal_words(w2w, w2w_raw)
-        deal_scales(w2s, w2s_raw)
+        deal_scales(w2s, w2s_raw, 0, PACK)
 
-        def product(name, ww, ws, codes, scales, t, c):
-            acc = ps.tile([P, CH], F32, name="%s%d_%d" % (name, t, c), tag="bank%d_%d" % (t, c))
+        def product(acc, t, words, scales, codes, code_scales):
             nc.tensor.matmul_mx(
                 out=acc[:],
-                lhsT=ww[:, 2 * P * t : 2 * P * (t + 1)].bitcast(FP4X4),
-                lhsT_scale=ws[:, P * t : P * (t + 1)],
+                lhsT=words[:, 2 * P * t : 2 * P * (t + 1)].bitcast(FP4X4),
+                lhsT_scale=scales[:, P * t : P * (t + 1)],
                 rhs=codes.bitcast(FP8X4),
-                rhs_scale=scales,
+                rhs_scale=code_scales,
                 start=True,
                 stop=True,
             )
-            return acc
 
+        halves = [slice(0, HALF), slice(HALF, S)]
+        y_win = tiles("y_win", [P, 2 * S], F32)
         y_ps = {}
-        y_win = tiles("y_win", PACK, [P, S], F32)
-        for c in range(HALVES):
-            for t in range(PACK):
-                y_ps[t, c] = product("y", w1w, w1s, xg[c][:], xsg[:, c * CH : (c + 1) * CH], t, c)
-                nc.scalar.copy(y_win[t][:, c * CH : (c + 1) * CH], y_ps[t, c][:])
+        for pair in range(0, PACK, 2):
+            for c in range(2):
+                for t in (pair, pair + 1):
+                    y_ps[t, c] = ps.tile([P, HALF], F32, name="y%d_%d" % (t, c), tag="bank%d_%d" % (t, c))
+                    product(y_ps[t, c], t, w1w, w1s, xg[c][:], xsg[:, halves[c]])
+                    nc.scalar.copy(y_win[t][:, halves[c]], y_ps[t, c][:])
 
-        gy = tiles("gy", HALVES, [P, PACK, CH], F32)
-        a_win = tiles("a_win", PACK, [P, S], F32)
-        a_own = tiles("a_own", HALVES, [P, PACK, CH], F32)
-        for c in range(HALVES):
-            for t in range(PACK):
-                nc.scalar.activation(gy[c][:, t, :], y_ps[t, c][:], ACT.Copy, scale=gain[:, t : t + 1])
-        for c in range(HALVES):
-            for t in range(PACK):
-                nc.scalar.activation(a_win[t][:, c * CH : (c + 1) * CH], y_ps[t, c][:], ACT.Abs)
-                nc.scalar.activation(a_own[c][:, t, :], y_ps[t, c][:], ACT.Abs)
+        gy = sb.tile([P, PACK, S], F32, name="gy")
+        a_win = tiles("a_win", [P, 2 * S], F32)
+        a_own = tiles("a_own", [P, S], F32)
 
-        y2 = tiles("y2_", HALVES, [P, PACK, CH], F32)
-        diff = tiles("diff", HALVES, [P, PACK, CH], F32)
-        zb = tiles("zb", HALVES, [P, PACK * CH], BF16)
-        zq = tiles("zq", HALVES, [P, CH], U32)
-        zs = tiles("zs", HALVES, [P, CH], U8)
-        h_win = tiles("h_win", PACK, [P, S], F32)
-        h_own = tiles("h_own", HALVES, [P, PACK, CH], F32)
+        def sizes(t):
+            nc.scalar.activation(a_win[t][:, 0:S], y_win[t][:, 0:S], ACT.Abs)
+            nc.scalar.activation(a_own[t][:], y_win[t][:, 0:S], ACT.Abs)
 
-        def second_product(c):
-            nc.vector.quantize_mx(out=zq[c][:].bitcast(FP8X4), scales=zs[c][:], in_=zb[c][:])
-            for t in range(PACK):
-                acc = product("h", w2w, w2s, zq[c][:], zs[c][:], t, c)
-                nc.scalar.activation(h_win[t][:, c * CH : (c + 1) * CH], acc[:], ACT.Copy, scale=-1.0)
-                nc.scalar.copy(h_own[c][:, t, :], acc[:])
+        sizes(0)
+        for t in range(PACK):
+            nc.scalar.activation(gy[:, t, :], y_win[t][:, 0:S], ACT.Copy, scale=gain[:, t : t + 1])
+        for t in range(1, PACK):
+            sizes(t)
 
-        for c in range(HALVES):
-            for t in range(PACK):
-                nc.vector.tensor_copy(y2[c][:, t, :], y_win[t][:].indirect(part(n2_t, c)))
-                if t == 0 and c > 0:
-                    second_product(c - 1)
-                if t > 0:
-                    nc.vector.tensor_tensor(diff[c][:, t - 1, :], y_win[t - 1][:].indirect(part(n1_t, c)), y2[c][:, t - 1, :], ALU.subtract)
-            nc.vector.tensor_tensor(diff[c][:, PACK - 1, :], y_win[PACK - 1][:].indirect(part(n1_t, c)), y2[c][:, PACK - 1, :], ALU.subtract)
-            nc.vector.tensor_tensor(paired_out(zb[c][:]), paired_in(diff[c][:]), paired_in(gy[c][:]), ALU.mult)
+        y2 = tiles("y2_", [P, S], F32)
+        diff = sb.tile([P, PACK, S], F32, name="diff", tag="diff_then_den")
+        for pair in range(0, PACK, 2):
+            for t in (pair, pair + 1):
+                nc.vector.tensor_copy(y2[t][:], y_win[t][:].indirect(n2_t[:]))
+            for t in (pair, pair + 1):
+                nc.vector.tensor_tensor(diff[:, t, :], y_win[t][:].indirect(n1_t[:]), y2[t][:], ALU.subtract)
 
-        den = tiles("den", HALVES, [P, PACK, CH], F32)
-        root = tiles("root", HALVES, [P, PACK, CH], F32)
-        inv = tiles("inv", HALVES, [P, PACK, CH], F32)
-        for c in range(HALVES):
-            for t in range(PACK):
-                nc.vector.tensor_tensor(den[c][:, t, :], a_win[t][:].indirect(part(n4_t, c)), a_own[c][:, t, :], ALU.add)
-                if t == 0 and c == 0:
-                    second_product(HALVES - 1)
-            nc.scalar.activation(root[c][:], den[c][:], ACT.Abs_reciprocal_sqrt, bias=0.5)
-            nc.scalar.activation(inv[c][:], root[c][:], ACT.Square)
+        den_lo = sb.tile([P, 2, S], F32, name="den_lo")
+        den = [den_lo[:, 0, :], den_lo[:, 1, :]]
+        root = tiles("root", [P, S], F32)
+        inv = tiles("inv", [P, S], F32)
 
-        num = tiles("num", HALVES, [P, PACK, CH], F32)
-        res = tiles("res", HALVES, [P, PACK, CH], F32)
-        ob = tiles("ob", HALVES, [P, PACK * CH], BF16)
-        oq = tiles("oq", HALVES, [P, CH], U32)
-        osc = sb.tile([P, S], U8, name="osc", align_bytes=64)
+        def denominator(t):
+            nc.vector.tensor_tensor(den[t], a_win[t][:].indirect(n4_t[:]), a_own[t][:], ALU.add)
+
+        def inverse_root(t):
+            nc.scalar.activation(root[t][:], den[t], ACT.Abs_reciprocal_sqrt, bias=0.5)
+
+        def inverse(t):
+            nc.scalar.activation(inv[t][:], root[t][:], ACT.Square)
+
+        zb = sb.tile([P, PACK * S], BF16, name="zb", align_bytes=64)
+        zq = sb.tile([P, S], U32, name="zq", align_bytes=64)
+        zs = sb.tile([P, S], U8, name="zs", align_bytes=64)
+        denominator(0)
+        nc.vector.tensor_tensor(paired_out(zb[:]), paired_in(diff[:]), paired_in(gy[:]), ALU.mult)
+        denominator(1)
+        nc.vector.quantize_mx(out=zq[:].bitcast(FP8X4), scales=zs[:], in_=zb[:])
+        den_hi = sb.tile([P, 2, S], F32, name="den_hi", tag="diff_then_den")
+        den.extend([den_hi[:, 0, :], den_hi[:, 1, :]])
+        denominator(2)
+        denominator(3)
+
+        h_win = tiles("h_win", [P, 2 * S], F32)
+        h_own = tiles("h_own", [P, S], F32)
+
+        def second_product(t):
+            acc = ps.tile([P, S], F32, name="h%d" % t, tag="bank%d_0" % t)
+            product(acc, t, w2w, w2s, zq[:], zs[:])
+            nc.scalar.activation(h_win[t][:, 0:S], acc[:], ACT.Copy, scale=-1.0)
+            nc.scalar.copy(h_own[t][:], acc[:])
+
+        inverse_root(0)
+        inverse_root(1)
+        second_product(0)
+        second_product(1)
+        inverse(0)
+        second_product(2)
+        inverse(1)
+        second_product(3)
+        for t in (2, 3):
+            inverse_root(t)
+            inverse(t)
+
+        num = tiles("num", [P, S], F32)
+        res = sb.tile([P, PACK, S], F32, name="res")
         out_rows = out_0.rearrange("(p t) j -> p t j", t=PACK)
+
+        def result(t):
+            nc.vector.tensor_tensor(res[:, t, :], num[t][:], inv[t][:], ALU.mult)
+            nc.sync.dma_start(out=out_rows[:, t, :], in_=res[:, t, :])
+
+        for t in range(PACK):
+            nc.vector.tensor_tensor(num[t][:], h_win[t][:].indirect(n3_t[:]), h_own[t][:], ALU.add)
+            if t > 0:
+                result(t - 1)
+        result(PACK - 1)
+
+        osc = sb.tile([P, S], U8, name="osc", align_bytes=64)
         out_words = out_1[0].rearrange("p n t -> p (n t)").bitcast(I32)
-
-        def planes(c):
-            nc.vector.quantize_mx(out=oq[c][:].bitcast(FP8X4), scales=osc[:, c * CH : (c + 1) * CH], in_=ob[c][:])
-            nc.sync.dma_start(out=out_words[:, c * CH : (c + 1) * CH], in_=oq[c][:].bitcast(I32))
-
-        for c in range(HALVES):
-            for t in range(PACK):
-                nc.vector.tensor_tensor(num[c][:, t, :], h_win[t][:].indirect(part(n3_t, c)), h_own[c][:, t, :], ALU.add)
-            if c > 0:
-                planes(c - 1)
-            nc.vector.tensor_tensor(res[c][:], num[c][:], inv[c][:], ALU.mult)
-            nc.sync.dma_start(out=out_rows[:, :, c * CH : (c + 1) * CH], in_=res[c][:])
-            nc.scalar.copy(paired_out(ob[c][:]), paired_in(res[c][:]))
-        planes(HALVES - 1)
+        ob = [sb.tile([P, PACK * HALF], BF16, name="ob%d" % c, align_bytes=64) for c in range(2)]
+        nc.vector.tensor_copy(paired_out(ob[0][:]), paired_in(res[:, :, 0:HALF]))
+        nc.scalar.copy(paired_out(ob[1][:]), paired_in(res[:, :, HALF:S]))
+        for c in range(2):
+            cols = slice(c * HALF, (c + 1) * HALF)
+            oq = sb.tile([P, HALF], U32, name="oq%d" % c, align_bytes=64)
+            nc.vector.quantize_mx(out=oq[:].bitcast(FP8X4), scales=osc[:, cols], in_=ob[c][:])
+            nc.sync.dma_start(out=out_words[:, cols], in_=oq[:].bitcast(I32))
         for q in range(4):
             queue = nc.sync if q % 2 else nc.scalar
             queue.dma_start(out=out_2[0, 4 * q : 4 * q + 4, :].bitcast(I32), in_=osc[32 * q : 32 * q + 4, :].bitcast(I32))

@@ -21,17 +21,17 @@ PACK = 4
 HALF = S // 2
 
 
-def load_scale_rows(queue, tile, scales):
+def load_scale_rows(queues, tile, scales):
     for q in range(4):
-        queue.dma_start(out=tile[32 * q : 32 * q + 4, :].bitcast(I32), in_=scales[0, 4 * q : 4 * q + 4, :].bitcast(I32))
+        queues[q % len(queues)].dma_start(out=tile[32 * q : 32 * q + 4, :].bitcast(I32), in_=scales[0, 4 * q : 4 * q + 4, :].bitcast(I32))
 
 
 def paired_in(ap):
-    return ap.rearrange("p t (c i) -> p c t i", i=2)
+    return ap.rearrange("p t (c i) -> p c t i", i=4)
 
 
 def paired_out(ap):
-    return ap.rearrange("p (c i t) -> p c t i", i=2, t=PACK)
+    return ap.rearrange("p (c i t) -> p c t i", i=4, t=PACK)
 
 
 def tile_picked_skipnormbwind_none_po_kernel(
@@ -64,18 +64,18 @@ def tile_picked_skipnormbwind_none_po_kernel(
         nc.vector.memset(w1s_raw[:].bitcast(I32), 0)
         nc.gpsimd.memset(w2s_raw[:].bitcast(I32), 0)
         nc.vector.memset(warm_in[:], 1.0)
-        nc.scalar.activation(warm_out[:], warm_in[:], ACT.Abs_reciprocal_sqrt)
 
-        load_scale_rows(nc.sync, xs, x_scales)
+        load_scale_rows((nc.sync, nc.scalar), xs, x_scales)
+        nc.scalar.activation(warm_out[:], warm_in[:], ACT.Abs_reciprocal_sqrt)
         nc.sync.dma_start(offs_t[:], offs)
         nc.sync.dma_start(out=w1w_raw[:].bitcast(I32), in_=w1_words[0].bitcast(I32))
         nc.sync.dma_start(n2_t[:], n2)
         nc.sync.dma_start(out=xw[:].bitcast(I32), in_=x_words[0].rearrange("p n t -> p (n t)").bitcast(I32))
-        load_scale_rows(nc.sync, w1s_raw, w1_scales)
+        load_scale_rows((nc.sync,), w1s_raw, w1_scales)
         nc.sync.dma_start(out=w2w_raw[:].bitcast(I32), in_=w2_words[0].bitcast(I32))
         nc.sync.dma_start(n1_t[:], n1)
         nc.sync.dma_start(out=gain[:], in_=gn.rearrange("(p t) o -> p (t o)", t=PACK))
-        load_scale_rows(nc.sync, w2s_raw, w2_scales)
+        load_scale_rows((nc.sync,), w2s_raw, w2_scales)
         nc.sync.dma_start(n4_t[:], n4)
         nc.sync.dma_start(n3_t[:], n3)
 

from contextlib import ExitStack

import concourse.mybir as mybir

K, T, S, H, N = 512, 2048, 512, 512, 512
FLOPS = 2 * K * H * S + 2 * H * N * S

F32 = mybir.dt.float32
BF16 = mybir.dt.bfloat16
I32 = mybir.dt.int32
U32 = mybir.dt.uint32
U16 = mybir.dt.uint16
U8 = mybir.dt.uint8
FP8X4 = mybir.dt.float8_e4m3fn_x4
FP4X4 = mybir.dt.float4_e2m1fn_x4
ALU = mybir.AluOpType
ACT = mybir.ActivationFunctionType

P = 128
PACK = 4
HALF = S // 2


def load_scale_rows(queues, tile, scales):
    for q in range(4):
        queues[q % len(queues)].dma_start(out=tile[32 * q : 32 * q + 4, :].bitcast(I32), in_=scales[0, 4 * q : 4 * q + 4, :].bitcast(I32))


def paired_in(ap):
    return ap.rearrange("p t (c i) -> p c t i", i=4)


def paired_out(ap):
    return ap.rearrange("p (c i t) -> p c t i", i=4, t=PACK)


def tile_picked_skipnormbwind_none_po_kernel(
    tc, x_words, x_scales, w1_words, w1_scales, gn, w2_words, w2_scales, offs, n1, n2, n3, n4, out_0, out_1, out_2
):
    nc = tc.nc
    with ExitStack() as ctx:
        sb = ctx.enter_context(tc.tile_pool(name="sb", bufs=1))
        ps = ctx.enter_context(tc.psum_pool(name="ps", bufs=1))

        def tiles(name, shape, dtype):
            return [sb.tile(shape, dtype, name="%s%d" % (name, t), align_bytes=64) for t in range(PACK)]

        offs_t = sb.tile([P, S // 16], U16, name="offs_t")
        n1_t = sb.tile([P, S // 16], U16, name="n1_t")
        n2_t = sb.tile([P, S // 16], U16, name="n2_t")
        n3_t = sb.tile([P, S // 16], U16, name="n3_t")
        n4_t = sb.tile([P, S // 16], U16, name="n4_t")
        xw = sb.tile([P, T], U32, name="xw", align_bytes=64)
        xs = sb.tile([P, T], U8, name="xs", align_bytes=64)
        w1w_raw = sb.tile([P, 2 * H], U8, name="w1w_raw", align_bytes=64)
        w2w_raw = sb.tile([P, 2 * N], U8, name="w2w_raw", align_bytes=64)
        w1s_raw = sb.tile([P, H], U8, name="w1s_raw", align_bytes=64)
        w2s_raw = sb.tile([P, N], U8, name="w2s_raw", align_bytes=64)
        gain = sb.tile([P, PACK], F32, name="gain")
        warm_in = sb.tile([P, 1], F32, name="warm_in")
        warm_out = sb.tile([P, 1], F32, name="warm_out")

        nc.vector.memset(xs[:].bitcast(I32), 0)
        nc.vector.memset(w1s_raw[:].bitcast(I32), 0)
        nc.gpsimd.memset(w2s_raw[:].bitcast(I32), 0)
        nc.vector.memset(warm_in[:], 1.0)

        load_scale_rows((nc.sync, nc.scalar), xs, x_scales)
        nc.scalar.activation(warm_out[:], warm_in[:], ACT.Abs_reciprocal_sqrt)
        nc.sync.dma_start(offs_t[:], offs)
        nc.sync.dma_start(out=w1w_raw[:].bitcast(I32), in_=w1_words[0].bitcast(I32))
        nc.sync.dma_start(n2_t[:], n2)
        nc.sync.dma_start(out=xw[:].bitcast(I32), in_=x_words[0].rearrange("p n t -> p (n t)").bitcast(I32))
        load_scale_rows((nc.sync,), w1s_raw, w1_scales)
        nc.sync.dma_start(out=w2w_raw[:].bitcast(I32), in_=w2_words[0].bitcast(I32))
        nc.sync.dma_start(n1_t[:], n1)
        nc.sync.dma_start(out=gain[:], in_=gn.rearrange("(p t) o -> p (t o)", t=PACK))
        load_scale_rows((nc.sync,), w2s_raw, w2_scales)
        nc.sync.dma_start(n4_t[:], n4)
        nc.sync.dma_start(n3_t[:], n3)

        def deal_words(dst, src):
            nc.vector.tensor_copy(
                out=dst[:].rearrange("p (t m b) -> p t m b", t=PACK, b=2),
                in_=src[:].rearrange("p (m t b) -> p t m b", t=PACK, b=2),
            )

        def deal_scales(dst, src, t0, t1):
            nc.vector.tensor_copy(
                out=dst[:].rearrange("p (t m) -> p t m", t=PACK)[:, t0:t1, :],
                in_=src[:].rearrange("p (m t) -> p t m", t=PACK)[:, t0:t1, :],
            )

        xsg = sb.tile([P, S], U8, name="xsg", align_bytes=64)
        xg = [sb.tile([P, HALF], U32, name="xg%d" % c, align_bytes=64) for c in range(2)]
        w1w = sb.tile([P, 2 * H], U8, name="w1w", align_bytes=64)
        w2w = sb.tile([P, 2 * N], U8, name="w2w", align_bytes=64)
        w1s = sb.tile([P, H], U8, name="w1s", align_bytes=64)
        w2s = sb.tile([P, N], U8, name="w2s", align_bytes=64)
        nc.vector.tensor_copy(xsg[:], xs[:].indirect(offs_t[:]))
        deal_words(w1w, w1w_raw)
        nc.vector.tensor_copy(xg[0][:], xw[:].indirect(offs_t[:, 0 : HALF // 16]))
        deal_scales(w1s, w1s_raw, 0, 2)
        nc.vector.tensor_copy(xg[1][:], xw[:].indirect(offs_t[:, HALF // 16 : S // 16]))
        deal_scales(w1s, w1s_raw, 2, PACK)
        deal_words(w2w, w2w_raw)
        deal_scales(w2s, w2s_raw, 0, PACK)

        def product(acc, t, words, scales, codes, code_scales):
            nc.tensor.matmul_mx(
                out=acc[:],
                lhsT=words[:, 2 * P * t : 2 * P * (t + 1)].bitcast(FP4X4),
                lhsT_scale=scales[:, P * t : P * (t + 1)],
                rhs=codes.bitcast(FP8X4),
                rhs_scale=code_scales,
                start=True,
                stop=True,
            )

        halves = [slice(0, HALF), slice(HALF, S)]
        y_win = tiles("y_win", [P, 2 * S], F32)
        y_ps = {}
        for pair in range(0, PACK, 2):
            for c in range(2):
                for t in (pair, pair + 1):
                    y_ps[t, c] = ps.tile([P, HALF], F32, name="y%d_%d" % (t, c), tag="bank%d_%d" % (t, c))
                    product(y_ps[t, c], t, w1w, w1s, xg[c][:], xsg[:, halves[c]])
                    nc.scalar.copy(y_win[t][:, halves[c]], y_ps[t, c][:])

        gy = sb.tile([P, PACK, S], F32, name="gy")
        a_win = tiles("a_win", [P, 2 * S], F32)
        a_own = tiles("a_own", [P, S], F32)

        def sizes(t):
            nc.scalar.activation(a_win[t][:, 0:S], y_win[t][:, 0:S], ACT.Abs)
            nc.scalar.activation(a_own[t][:], y_win[t][:, 0:S], ACT.Abs)

        sizes(0)
        for t in range(PACK):
            nc.scalar.activation(gy[:, t, :], y_win[t][:, 0:S], ACT.Copy, scale=gain[:, t : t + 1])
        for t in range(1, PACK):
            sizes(t)

        y2 = tiles("y2_", [P, S], F32)
        diff = sb.tile([P, PACK, S], F32, name="diff", tag="diff_then_den")
        for pair in range(0, PACK, 2):
            for t in (pair, pair + 1):
                nc.vector.tensor_copy(y2[t][:], y_win[t][:].indirect(n2_t[:]))
            for t in (pair, pair + 1):
                nc.vector.tensor_tensor(diff[:, t, :], y_win[t][:].indirect(n1_t[:]), y2[t][:], ALU.subtract)

        den_lo = sb.tile([P, 2, S], F32, name="den_lo")
        den = [den_lo[:, 0, :], den_lo[:, 1, :]]
        root = tiles("root", [P, S], F32)
        inv = tiles("inv", [P, S], F32)

        def denominator(t):
            nc.vector.tensor_tensor(den[t], a_win[t][:].indirect(n4_t[:]), a_own[t][:], ALU.add)

        def inverse_root(t):
            nc.scalar.activation(root[t][:], den[t], ACT.Abs_reciprocal_sqrt, bias=0.5)

        def inverse(t):
            nc.scalar.activation(inv[t][:], root[t][:], ACT.Square)

        zb = sb.tile([P, PACK * S], BF16, name="zb", align_bytes=64)
        zq = sb.tile([P, S], U32, name="zq", align_bytes=64)
        zs = sb.tile([P, S], U8, name="zs", align_bytes=64)
        denominator(0)
        nc.vector.tensor_tensor(paired_out(zb[:]), paired_in(diff[:]), paired_in(gy[:]), ALU.mult)
        denominator(1)
        nc.vector.quantize_mx(out=zq[:].bitcast(FP8X4), scales=zs[:], in_=zb[:])
        den_hi = sb.tile([P, 2, S], F32, name="den_hi", tag="diff_then_den")
        den.extend([den_hi[:, 0, :], den_hi[:, 1, :]])
        denominator(2)
        denominator(3)

        h_win = tiles("h_win", [P, 2 * S], F32)
        h_own = tiles("h_own", [P, S], F32)

        def second_product(t):
            acc = ps.tile([P, S], F32, name="h%d" % t, tag="bank%d_0" % t)
            product(acc, t, w2w, w2s, zq[:], zs[:])
            nc.scalar.activation(h_win[t][:, 0:S], acc[:], ACT.Copy, scale=-1.0)
            nc.scalar.copy(h_own[t][:], acc[:])

        inverse_root(0)
        inverse_root(1)
        second_product(0)
        second_product(1)
        inverse(0)
        second_product(2)
        inverse(1)
        second_product(3)
        for t in (2, 3):
            inverse_root(t)
            inverse(t)

        num = tiles("num", [P, S], F32)
        res = sb.tile([P, PACK, S], F32, name="res")
        out_rows = out_0.rearrange("(p t) j -> p t j", t=PACK)

        def result(t):
            nc.vector.tensor_tensor(res[:, t, :], num[t][:], inv[t][:], ALU.mult)
            nc.sync.dma_start(out=out_rows[:, t, :], in_=res[:, t, :])

        for t in range(PACK):
            nc.vector.tensor_tensor(num[t][:], h_win[t][:].indirect(n3_t[:]), h_own[t][:], ALU.add)
            if t > 0:
                result(t - 1)
        result(PACK - 1)

        osc = sb.tile([P, S], U8, name="osc", align_bytes=64)
        out_words = out_1[0].rearrange("p n t -> p (n t)").bitcast(I32)
        ob = [sb.tile([P, PACK * HALF], BF16, name="ob%d" % c, align_bytes=64) for c in range(2)]
        nc.vector.tensor_copy(paired_out(ob[0][:]), paired_in(res[:, :, 0:HALF]))
        nc.scalar.copy(paired_out(ob[1][:]), paired_in(res[:, :, HALF:S]))
        for c in range(2):
            cols = slice(c * HALF, (c + 1) * HALF)
            oq = sb.tile([P, HALF], U32, name="oq%d" % c, align_bytes=64)
            nc.vector.quantize_mx(out=oq[:].bitcast(FP8X4), scales=osc[:, cols], in_=ob[c][:])
            nc.sync.dma_start(out=out_words[:, cols], in_=oq[:].bitcast(I32))
        for q in range(4):
            queue = nc.sync if q % 2 else nc.scalar
            queue.dma_start(out=out_2[0, 4 * q : 4 * q + 4, :].bitcast(I32), in_=osc[32 * q : 32 * q + 4, :].bitcast(I32))
